import numpy as np
import ml_dtypes


def mxq(x, axis, fmt="e4m3"):
    dtype, down = {"e4m3": (ml_dtypes.float8_e4m3fn, 7), "e5m2": (ml_dtypes.float8_e5m2, 14)}[fmt]
    v = np.moveaxis(np.asarray(x, np.float32).astype(ml_dtypes.bfloat16).astype(np.float64), axis, -1)
    blocks = v.reshape(v.shape[:-1] + (-1, 32))
    amax = np.abs(blocks).max(-1, keepdims=True)
    byte = np.maximum(np.where(amax > 0, np.frexp(amax)[1] - 1 + 127, 0) - down, 1)
    scale = np.exp2(byte - 127.0)
    codes = (blocks / scale).astype(np.float32).astype(dtype).astype(np.float64)
    return np.moveaxis((codes * scale).reshape(v.shape), -1, axis)


WIDE = False


def mx_kscale(k):
    if not WIDE:
        return np.ones(k)
    levels = np.array([10, -10, 5, -5, 0])
    if k % 512:
        return np.exp2(np.random.permutation(np.resize(levels, k // 32))).repeat(32)
    a = np.empty((k // 512, 16))
    for p in range(k // 512):
        a[p, :8] = np.random.permutation(np.resize(levels, 8))
        for g in range(8):
            far = levels[np.abs(levels - a[p, g]) >= 10]
            a[p, g + 8] = far[np.random.randint(len(far))]
    return np.exp2(a.ravel()).repeat(32)


def f64(x):
    return np.asarray(x).astype(np.float64)


def striped(idx):
    return np.tile(idx.reshape(-1, 16).T, (8, 1)).astype(np.uint16)


def unstriped(offs):
    return offs[:16].T.reshape(-1).astype(np.int64)


E2M1 = np.array([0.0, 0.5, 1.0, 1.5, 2.0, 3.0, 4.0, 6.0, -0.0, -0.5, -1.0, -1.5, -2.0, -3.0, -4.0, -6.0])


def pack_weight(w, fmt):
    k, n = w.shape
    w = f64(np.asarray(w, np.float32).astype(ml_dtypes.bfloat16)).reshape(k // 32, 32, n)
    amax = np.abs(w).max(1)
    if fmt == "e4m3":
        byte = np.frexp(amax)[1] - 1 + 127 - 7
    else:
        mant, ex = np.frexp(amax / 6.0)
        byte = np.where(mant > 0.5, ex, ex - 1) + 127
    byte = np.clip(np.where(amax > 0, byte, 1), 1, 254)
    scaled = (w * np.exp2(127.0 - byte)[:, None, :]).reshape(k, n).astype(np.float32)
    by_word = np.ascontiguousarray(scaled.reshape(k // 512, 128, 4, n).transpose(0, 1, 3, 2))
    if fmt == "e4m3":
        words = by_word.astype(ml_dtypes.float8_e4m3fn).view(np.uint8)
    else:
        c = by_word.astype(ml_dtypes.float4_e2m1fn).view(np.uint8) & 0xF
        words = (c[..., 0::2] | (c[..., 1::2] << 4)).reshape(k // 512, 128, 2 * n)
    return np.ascontiguousarray(words), np.ascontiguousarray(byte.astype(np.uint8).reshape(k // 512, 16, n))


def unpack_weight(words, scales, fmt):
    g, _, n = scales.shape
    words = np.ascontiguousarray(words).reshape(g, 128, n, -1)
    if fmt == "e4m3":
        vals = words.view(ml_dtypes.float8_e4m3fn).astype(np.float64)
    else:
        nib = np.empty((g, 128, n, 4), np.uint8)
        nib[..., 0::2] = words & 0xF
        nib[..., 1::2] = words >> 4
        vals = E2M1[nib]
    vals = vals * np.repeat(np.exp2(scales.astype(np.float64) - 127.0), 8, axis=1)[..., None]
    return vals.transpose(0, 1, 3, 2).reshape(g * 512, n)


def gelu(v):
    return 0.5 * v * (1.0 + np.tanh(np.sqrt(2.0 / np.pi) * (v + 0.044715 * v**3)))


T, S, T2, P, K, H, N = 4096, 1024, 2048, 1024, 1024, 1024, 512


def setup_inputs():
    n = np.random.standard_normal
    s = mx_kscale(K)[:, None]
    u = mx_kscale(H)[:, None]
    tab_words, tab_scales = pack_weight(n((K, T)) * s, "e4m3")
    w2_words, w2_scales = pack_weight(1.3 * n((H, N)) / np.sqrt(H) / u, "e2m1")
    return {
        "tab_words": tab_words,
        "tab_scales": tab_scales,
        "offs": striped(np.random.permutation(T)[:S]),
        "w1": (n((K, H)) / np.sqrt(K) / s * u.T).astype(np.float32),
        "page0": (n((H, T2)) * u).astype(np.float32),
        "offs2": striped(np.random.permutation(T2)[:S]),
        "offs3": striped(np.random.permutation(T2)[:P]),
        "w2_words": w2_words,
        "w2_scales": w2_scales,
    }


def reference(tab_words, tab_scales, offs, w1, page0, offs2, offs3, w2_words, w2_scales):
    v = unpack_weight(tab_words, tab_scales, "e4m3")[:, unstriped(offs)]
    w1q = mxq(f64(w1), 0, "e4m3")
    h = w1q.T @ v
    page = f64(page0).copy()
    l2 = unstriped(offs2)
    page[:, l2] = np.maximum(page[:, l2], h)
    x = page[:, unstriped(offs3)]
    w2 = unpack_weight(w2_words, w2_scales, "e2m1")
    y = w2.T @ mxq(x, 0, "e4m3")
    return np.tanh(y)

@@ -1,0 +1,213 @@
+from contextlib import ExitStack
+
+import concourse.mybir as mybir
+
+T, S, T2, NX, K, H, N = 4096, 1024, 2048, 1024, 1024, 1024, 512
+FLOPS = 2 * K * H * S + 2 * H * N * NX
+
+F32 = mybir.dt.float32
+BF16 = mybir.dt.bfloat16
+I32 = mybir.dt.int32
+U32 = mybir.dt.uint32
+U16 = mybir.dt.uint16
+U8 = mybir.dt.uint8
+FP8X4 = mybir.dt.float8_e4m3fn_x4
+FP4X4 = mybir.dt.float4_e2m1fn_x4
+MAX = mybir.AluOpType.max
+TANH = mybir.ActivationFunctionType.Tanh
+
+P = 128
+PACK = 4
+K_PASS = P * PACK
+BANK = 512
+PER_COLUMN = 16
+PIECES = (256, 256, 256, 128, 128)
+RING = 3
+
+
+def tile_list_bearing_seizure_step_kernel(
+    tc, tab_words, tab_scales, offs, w1, page0, offs2, offs3, w2_words, w2_scales, out
+):
+    nc = tc.nc
+    k_passes = K // K_PASS
+    r_passes = H // K_PASS
+    n_tiles = N // P
+    page_tiles = r_passes * PACK
+
+    with ExitStack() as ctx:
+        keep = ctx.enter_context(tc.tile_pool(name="keep", bufs=1))
+        stage = ctx.enter_context(tc.tile_pool(name="stage", bufs=2))
+        psum = ctx.enter_context(tc.psum_pool(name="psum", bufs=4))
+
+        idx = keep.tile([P, S // PER_COLUMN], U16, name="idx")
+        idx2 = keep.tile([P, S // PER_COLUMN], U16, name="idx2")
+        idx3 = keep.tile([P, NX // PER_COLUMN], U16, name="idx3")
+        table = [keep.tile([P, T], I32, name=f"table{a}", align_bytes=64) for a in range(k_passes)]
+        table_scales = keep.tile([P, T], U8, name="table_scales", align_bytes=64)
+        v_codes = [keep.tile([P, S], U32, name=f"v_codes{a}", align_bytes=64) for a in range(k_passes)]
+        v_scales = keep.tile([P, S], U8, name="v_scales", align_bytes=64)
+        w1_codes = {}
+        w1_scales = {}
+        for a in range(k_passes):
+            for b in range(r_passes):
+                w1_codes[a, b] = keep.tile([P, K_PASS], U32, name=f"w1_codes{a}{b}", align_bytes=64)
+                w1_scales[a, b] = keep.tile([P, K_PASS], U8, name=f"w1_scales{a}{b}", align_bytes=64)
+        page = [keep.tile([P, T2], F32, name=f"page{i}", align_bytes=64) for i in range(page_tiles)]
+        w2_codes = keep.tile([P, r_passes, 2 * N], U8, name="w2_codes", align_bytes=64)
+        w2_planes = keep.tile([P, r_passes, N], U8, name="w2_planes", align_bytes=64)
+        x_codes = [keep.tile([P, NX], U32, name=f"x_codes{b}", align_bytes=64) for b in range(r_passes)]
+        x_scales = [keep.tile([P, NX], U8, name=f"x_scales{b}", align_bytes=64) for b in range(r_passes)]
+        x_rows_first = keep.tile([P, PACK, NX], BF16, name="x_rows_first", align_bytes=64)
+        x_woven_first = keep.tile([P, NX * PACK], BF16, name="x_woven_first", align_bytes=64)
+
+        def ring_tile(slot, shape, dtype, name):
+            return keep.tile(shape, dtype, name=name, tag=f"ring{slot % RING}", align_bytes=64)
+
+        def load_table(a):
+            nc.sync.dma_start(out=table[a][:], in_=tab_words[a].rearrange("p t i -> p (t i)").bitcast(I32))
+
+        def load_page(i):
+            b, t = divmod(i, PACK)
+            rows = page0[b * K_PASS : (b + 1) * K_PASS, :].rearrange("(p t) c -> p t c", t=PACK)
+            nc.sync.dma_start(out=page[i][:], in_=rows[:, t, :])
+
+        def load_w1(a, b):
+            raw = stage.tile([P, PACK, K_PASS], F32, name="w1_raw", align_bytes=64)
+            block = w1[a * K_PASS : (a + 1) * K_PASS, b * K_PASS : (b + 1) * K_PASS]
+            nc.sync.dma_start(out=raw[:], in_=block.rearrange("(p j) c -> p j c", j=PACK))
+            return raw
+
+        def weave_w1(raw):
+            woven = stage.tile([P, K_PASS * PACK], BF16, name="w1_woven", align_bytes=64)
+            nc.scalar.copy(
+                out=woven[:].rearrange("p (t m j) -> p m j t", t=PACK, j=PACK),
+                in_=raw[:].rearrange("p j (m t) -> p m j t", t=PACK),
+            )
+            return woven
+
+        def quantize_w1(woven, a, b):
+            nc.vector.quantize_mx(out=w1_codes[a, b][:].bitcast(FP8X4), scales=w1_scales[a, b][:], in_=woven[:])
+
+        def weave_x(woven, rows):
+            nc.scalar.copy(
+                out=woven[:].rearrange("p (c i t) -> p c t i", i=4, t=PACK),
+                in_=rows[:].rearrange("p t (c i) -> p c t i", i=4),
+            )
+
+        def gather_x(rows, i, m0, width):
+            cols = slice(m0 // PER_COLUMN, (m0 + width) // PER_COLUMN)
+            nc.vector.tensor_copy(out=rows[:, i % PACK, :], in_=page[i][:].indirect(idx3[:, cols]))
+
+        def quantize_x(woven, b, m0, width):
+            nc.vector.quantize_mx(
+                out=x_codes[b][:, m0 : m0 + width].bitcast(FP8X4), scales=x_scales[b][:, m0 : m0 + width], in_=woven[:]
+            )
+
+        nc.vector.memset(table_scales[:].bitcast(I32), 0)
+        nc.vector.memset(w2_planes[:].rearrange("p a n -> p (a n)").bitcast(I32), 0)
+        nc.sync.dma_start(idx[:], offs)
+        load_table(0)
+        for q in range(4):
+            nc.scalar.dma_start(
+                out=table_scales[32 * q : 32 * q + 4 * k_passes, :].bitcast(I32),
+                in_=tab_scales[:, 4 * q : 4 * q + 4, :].bitcast(I32),
+            )
+        raws = [load_w1(a, 0) for a in range(k_passes)]
+        load_table(1)
+        nc.sync.dma_start(idx2[:], offs2)
+        load_page(0)
+        load_page(1)
+        nc.sync.dma_start(idx3[:], offs3)
+        load_page(2)
+        load_page(3)
+
+        nc.vector.tensor_copy(out=v_codes[0][:], in_=table[0][:].bitcast(U32).indirect(idx[:]))
+        nc.vector.tensor_copy(out=v_scales[:], in_=table_scales[:].indirect(idx[:]))
+        for a in range(k_passes):
+            quantize_w1(weave_w1(raws[a]), a, 0)
+        nc.vector.tensor_copy(out=v_codes[1][:], in_=table[1][:].bitcast(U32).indirect(idx[:]))
+
+        raws = [load_w1(a, 1) for a in range(k_passes)]
+        for i in range(PACK, page_tiles):
+            load_page(i)
+        nc.sync.dma_start(out=w2_codes[:].bitcast(I32), in_=w2_words.rearrange("a p c -> p a c").bitcast(I32))
+        for q in range(4):
+            nc.sync.dma_start(
+                out=w2_planes[32 * q : 32 * q + 4, :, :].bitcast(I32),
+                in_=w2_scales[:, 4 * q : 4 * q + 4, :].rearrange("a r c -> r a c").bitcast(I32),
+            )
+
+        def gather_old(i):
+            old = ring_tile(i, [P, S], F32, f"old{i}")
+            nc.vector.tensor_copy(out=old[:], in_=page[i][:].indirect(idx2[:]))
+            return old
+
+        def raise_to_h(old, i):
+            b, t = divmod(i, PACK)
+            for j0 in range(0, S, BANK):
+                cols = slice(j0, j0 + BANK)
+                h = psum.tile([P, BANK], F32, name="h")
+                for a in range(k_passes):
+                    nc.tensor.matmul_mx(
+                        out=h[:],
+                        lhsT=w1_codes[a, b][:, t * P : (t + 1) * P].bitcast(FP8X4),
+                        lhsT_scale=w1_scales[a, b][:, t * P : (t + 1) * P],
+                        rhs=v_codes[a][:, cols].bitcast(FP8X4),
+                        rhs_scale=v_scales[4 * a :, cols],
+                        start=(a == 0),
+                        stop=(a == k_passes - 1),
+                    )
+                nc.vector.tensor_tensor(out=old[:, cols], in0=old[:, cols], in1=h[:], op=MAX)
+
+        olds = {0: gather_old(0)}
+        for i in range(page_tiles):
+            if i + 1 < page_tiles:
+                olds[i + 1] = gather_old(i + 1)
+            raise_to_h(olds[i], i)
+            if 1 <= i <= PACK:
+                gather_x(x_rows_first, i - 1, 0, NX)
+            if i == PACK:
+                weave_x(x_woven_first, x_rows_first)
+            nc.vector.tensor_copy(out=page[i][:].indirect(idx2[:]), in_=olds[i][:])
+            if i == 1:
+                for a in range(k_passes):
+                    quantize_w1(weave_w1(raws[a]), a, 1)
+            if i == PACK + 1:
+                quantize_x(x_woven_first, 0, 0, NX)
+
+        out_v = out.rearrange("(c p) m -> p c m", p=P)
+
+        def finish(woven, m0, width):
+            quantize_x(woven, r_passes - 1, m0, width)
+            per_bank = BANK // width
+            res = stage.tile([P, n_tiles, width], F32, name="res", bufs=3)
+            for c0 in range(0, n_tiles, per_bank):
+                y = psum.tile([P, per_bank, width], F32, name="y")
+                for c in range(c0, c0 + per_bank):
+                    for b in range(r_passes):
+                        nc.tensor.matmul_mx(
+                            out=y[:, c - c0, :],
+                            lhsT=w2_codes[:, b, 2 * P * c : 2 * P * (c + 1)].bitcast(FP4X4),
+                            lhsT_scale=w2_planes[:, b, P * c : P * (c + 1)],
+                            rhs=x_codes[b][:, m0 : m0 + width].bitcast(FP8X4),
+                            rhs_scale=x_scales[b][:, m0 : m0 + width],
+                            start=(b == 0),
+                            stop=(b == r_passes - 1),
+                        )
+                nc.scalar.activation(out=res[:, c0 : c0 + per_bank, :], in_=y[:], func=TANH)
+            nc.sync.dma_start(out=out_v[:, :, m0 : m0 + width], in_=res[:])
+
+        first_slot = page_tiles - 2
+        waiting = None
+        m0 = 0
+        for n, width in enumerate(PIECES):
+            rows = ring_tile(first_slot - 2 * n, [P, PACK, width], BF16, f"x_rows{n}")
+            for i in range(PACK, page_tiles):
+                gather_x(rows, i, m0, width)
+            if waiting is not None:
+                finish(*waiting)
+            woven = ring_tile(first_slot - 2 * n - 1, [P, PACK * width], BF16, f"x_woven{n}")
+            weave_x(woven, rows)
+            waiting = (woven, m0, width)
+            m0 = m0 + width
+        finish(*waiting)

@@ -2,8 +2,8 @@ from contextlib import ExitStack
 
 import concourse.mybir as mybir
 
-T, S, T2, NX, K, H, N = 4096, 1024, 2048, 1024, 1024, 1024, 512
-FLOPS = 2 * K * H * S + 2 * H * N * NX
+T, S, T2, M, K, H, N = 4096, 1024, 2048, 1024, 1024, 1024, 512
+FLOPS = 2 * K * H * S + 2 * H * N * M
 
 F32 = mybir.dt.float32
 BF16 = mybir.dt.bfloat16
@@ -13,201 +13,283 @@ U16 = mybir.dt.uint16
 U8 = mybir.dt.uint8
 FP8X4 = mybir.dt.float8_e4m3fn_x4
 FP4X4 = mybir.dt.float4_e2m1fn_x4
-MAX = mybir.AluOpType.max
-TANH = mybir.ActivationFunctionType.Tanh
+ALU = mybir.AluOpType
+ACT = mybir.ActivationFunctionType
 
 P = 128
 PACK = 4
-K_PASS = P * PACK
+PASS = P * PACK
 BANK = 512
+QUADRANTS = 4
 PER_COLUMN = 16
-PIECES = (256, 256, 256, 128, 128)
-RING = 3
+ALIGN = 64
+
+DIRECT_TILES = (0, 1, 4)
+EARLY_TILES = 6
+PIECES = (256, 256, 128, 128, 128, 128)
+RUN = 4
+H_COPIES = 3
+CHOSEN_RING = 3
+TAKE_RING = 2
 
 
 def tile_list_bearing_seizure_step_kernel(
     tc, tab_words, tab_scales, offs, w1, page0, offs2, offs3, w2_words, w2_scales, out
 ):
     nc = tc.nc
-    k_passes = K // K_PASS
-    r_passes = H // K_PASS
+    k_passes = K // PASS
+    r_passes = H // PASS
     n_tiles = N // P
     page_tiles = r_passes * PACK
+    masked_tiles = [i for i in range(page_tiles) if i not in DIRECT_TILES]
 
     with ExitStack() as ctx:
         keep = ctx.enter_context(tc.tile_pool(name="keep", bufs=1))
         stage = ctx.enter_context(tc.tile_pool(name="stage", bufs=2))
-        psum = ctx.enter_context(tc.psum_pool(name="psum", bufs=4))
+        psum = ctx.enter_context(tc.psum_pool(name="psum", bufs=8))
 
         idx = keep.tile([P, S // PER_COLUMN], U16, name="idx")
         idx2 = keep.tile([P, S // PER_COLUMN], U16, name="idx2")
-        idx3 = keep.tile([P, NX // PER_COLUMN], U16, name="idx3")
-        table = [keep.tile([P, T], I32, name=f"table{a}", align_bytes=64) for a in range(k_passes)]
-        table_scales = keep.tile([P, T], U8, name="table_scales", align_bytes=64)
-        v_codes = [keep.tile([P, S], U32, name=f"v_codes{a}", align_bytes=64) for a in range(k_passes)]
-        v_scales = keep.tile([P, S], U8, name="v_scales", align_bytes=64)
-        w1_codes = {}
-        w1_scales = {}
-        for a in range(k_passes):
-            for b in range(r_passes):
-                w1_codes[a, b] = keep.tile([P, K_PASS], U32, name=f"w1_codes{a}{b}", align_bytes=64)
-                w1_scales[a, b] = keep.tile([P, K_PASS], U8, name=f"w1_scales{a}{b}", align_bytes=64)
-        page = [keep.tile([P, T2], F32, name=f"page{i}", align_bytes=64) for i in range(page_tiles)]
-        w2_codes = keep.tile([P, r_passes, 2 * N], U8, name="w2_codes", align_bytes=64)
-        w2_planes = keep.tile([P, r_passes, N], U8, name="w2_planes", align_bytes=64)
-        x_codes = [keep.tile([P, NX], U32, name=f"x_codes{b}", align_bytes=64) for b in range(r_passes)]
-        x_scales = [keep.tile([P, NX], U8, name=f"x_scales{b}", align_bytes=64) for b in range(r_passes)]
-        x_rows_first = keep.tile([P, PACK, NX], BF16, name="x_rows_first", align_bytes=64)
-        x_woven_first = keep.tile([P, NX * PACK], BF16, name="x_woven_first", align_bytes=64)
+        idx3 = keep.tile([P, M // PER_COLUMN], U16, name="idx3")
+        table = [keep.tile([P, T], I32, name=f"table{a}", tag=f"table{a}", align_bytes=ALIGN) for a in range(k_passes)]
+        table_scales = keep.tile([P, T], U8, name="table_scales", align_bytes=ALIGN)
+        v_codes = [keep.tile([P, S], U32, name=f"v_codes{a}", align_bytes=ALIGN) for a in range(k_passes)]
+        v_scales = keep.tile([P, S], U8, name="v_scales", align_bytes=ALIGN)
+        w1_codes = [keep.tile([P, k_passes * PASS], U32, name=f"w1_codes{b}", align_bytes=ALIGN) for b in range(r_passes)]
+        w1_scales = [keep.tile([P, k_passes * PASS], U8, name=f"w1_scales{b}", align_bytes=ALIGN) for b in range(r_passes)]
+        page = [keep.tile([P, T2], F32, name=f"page{i}", align_bytes=ALIGN) for i in range(page_tiles)]
+        w2_codes = keep.tile([P, r_passes, 2 * N], U8, name="w2_codes", align_bytes=ALIGN)
+        w2_planes = keep.tile([P, r_passes, N], U8, name="w2_planes", align_bytes=ALIGN)
+        x_codes = [keep.tile([P, M], U32, name=f"x_codes{b}", align_bytes=ALIGN) for b in range(r_passes)]
+        x_scales = [keep.tile([P, M], U8, name=f"x_scales{b}", align_bytes=ALIGN) for b in range(r_passes)]
 
-        def ring_tile(slot, shape, dtype, name):
-            return keep.tile(shape, dtype, name=name, tag=f"ring{slot % RING}", align_bytes=64)
+        def chosen_tag(i):
+            return f"chosen{masked_tiles.index(i) % CHOSEN_RING}"
+
+        def take_tag(i):
+            return f"take{masked_tiles.index(i) % TAKE_RING}"
+
+        def entries(lst, first, count):
+            return lst[:, first // PER_COLUMN : (first + count) // PER_COLUMN]
 
         def load_table(a):
             nc.sync.dma_start(out=table[a][:], in_=tab_words[a].rearrange("p t i -> p (t i)").bitcast(I32))
 
         def load_page(i):
             b, t = divmod(i, PACK)
-            rows = page0[b * K_PASS : (b + 1) * K_PASS, :].rearrange("(p t) c -> p t c", t=PACK)
+            rows = page0[b * PASS : (b + 1) * PASS, :].rearrange("(p t) c -> p t c", t=PACK)
             nc.sync.dma_start(out=page[i][:], in_=rows[:, t, :])
 
-        def load_w1(a, b):
-            raw = stage.tile([P, PACK, K_PASS], F32, name="w1_raw", align_bytes=64)
-            block = w1[a * K_PASS : (a + 1) * K_PASS, b * K_PASS : (b + 1) * K_PASS]
-            nc.sync.dma_start(out=raw[:], in_=block.rearrange("(p j) c -> p j c", j=PACK))
-            return raw
+        def load_w1(b):
+            raws = []
+            for a in range(k_passes):
+                raw = stage.tile([P, PACK, PASS], F32, name="w1_raw", align_bytes=ALIGN)
+                block = w1[a * PASS : (a + 1) * PASS, b * PASS : (b + 1) * PASS]
+                nc.sync.dma_start(out=raw[:], in_=block.rearrange("(p j) c -> p j c", j=PACK))
+                raws.append(raw)
+            return raws
 
-        def weave_w1(raw):
-            woven = stage.tile([P, K_PASS * PACK], BF16, name="w1_woven", align_bytes=64)
-            nc.scalar.copy(
-                out=woven[:].rearrange("p (t m j) -> p m j t", t=PACK, j=PACK),
-                in_=raw[:].rearrange("p j (m t) -> p m j t", t=PACK),
+        def quantize_w1(raws, b):
+            woven = keep.tile([P, k_passes * PASS * PACK], BF16, name=f"w1_woven{b}", tag="w1_woven", align_bytes=ALIGN)
+            for a, raw in enumerate(raws):
+                nc.scalar.copy(
+                    out=woven[:, a * PASS * PACK : (a + 1) * PASS * PACK].rearrange("p (t m j) -> p m j t", t=PACK, j=PACK),
+                    in_=raw[:].rearrange("p j (m t) -> p m j t", t=PACK),
+                )
+            nc.vector.quantize_mx(out=w1_codes[b][:].bitcast(FP8X4), scales=w1_scales[b][:], in_=woven[:])
+
+        def gather_words(a, j0, count):
+            nc.vector.tensor_copy(
+                out=v_codes[a][:, j0 : j0 + count], in_=table[a][:].bitcast(U32).indirect(entries(idx, j0, count))
             )
-            return woven
 
-        def quantize_w1(woven, a, b):
-            nc.vector.quantize_mx(out=w1_codes[a, b][:].bitcast(FP8X4), scales=w1_scales[a, b][:], in_=woven[:])
+        def gather_old(i):
+            old = keep.tile([P, S], F32, name=f"old{i}", align_bytes=ALIGN)
+            nc.vector.tensor_copy(out=old[:], in_=page[i][:].indirect(idx2[:]))
+            return old
+
+        def h_banks(i):
+            b, t = divmod(i, PACK)
+            banks = []
+            for j0 in range(0, S, BANK):
+                cols = slice(j0, j0 + BANK)
+                h = psum.tile([P, BANK], F32, name="h", tag="bank")
+                for a in range(k_passes):
+                    w1_cols = slice(a * PASS + t * P, a * PASS + (t + 1) * P)
+                    nc.tensor.matmul_mx(
+                        out=h[:],
+                        lhsT=w1_codes[b][:, w1_cols].bitcast(FP8X4),
+                        lhsT_scale=w1_scales[b][:, w1_cols],
+                        rhs=v_codes[a][:, cols].bitcast(FP8X4),
+                        rhs_scale=v_scales[PACK * a :, cols],
+                        start=(a == 0),
+                        stop=(a == k_passes - 1),
+                    )
+                banks.append((cols, h))
+            return banks
+
+        def max_on_vector(i):
+            for cols, h in h_banks(i):
+                nc.vector.tensor_tensor(out=olds[i][:, cols], in0=olds[i][:, cols], in1=h[:], op=ALU.max)
+
+        def make_masks(i):
+            h_copy = stage.tile([P, S], F32, name="h_copy", bufs=H_COPIES)
+            for cols, h in h_banks(i):
+                nc.scalar.copy(out=h_copy[:, cols], in_=h[:])
+            take = keep.tile([P, S], F32, name=f"take{i}", tag=take_tag(i), align_bytes=ALIGN)
+            stay = stage.tile([P, S], F32, name="stay")
+            nc.gpsimd.tensor_tensor(out=take[:], in0=h_copy[:], in1=olds[i][:], op=ALU.subtract)
+            nc.scalar.activation(out=take[:], in_=take[:], func=ACT.Sign)
+            nc.scalar.activation(out=take[:], in_=take[:], func=ACT.Relu)
+            nc.scalar.activation(out=stay[:], in_=take[:], func=ACT.Identity, scale=-1.0, bias=1.0)
+            return h_copy, take, stay
+
+        def choose(i, h_copy, take, stay):
+            nc.gpsimd.tensor_tensor(out=h_copy[:], in0=h_copy[:], in1=take[:], op=ALU.mult)
+            nc.gpsimd.tensor_tensor(out=olds[i][:], in0=olds[i][:], in1=stay[:], op=ALU.mult)
+            chosen = keep.tile([P, S], F32, name=f"chosen{i}", tag=chosen_tag(i), align_bytes=ALIGN)
+            nc.gpsimd.tensor_tensor(out=chosen[:], in0=h_copy[:], in1=olds[i][:], op=ALU.add)
+            return chosen
+
+        def gather_x(rows, i, m0, width):
+            nc.vector.tensor_copy(out=rows[:, i % PACK, :], in_=page[i][:].indirect(entries(idx3, m0, width)))
+
+        def scatter(i, values):
+            nc.vector.tensor_copy(out=page[i][:].indirect(idx2[:]), in_=values[:])
+            if i < PACK:
+                gather_x(x_rows_first, i, 0, M)
 
         def weave_x(woven, rows):
             nc.scalar.copy(
-                out=woven[:].rearrange("p (c i t) -> p c t i", i=4, t=PACK),
-                in_=rows[:].rearrange("p t (c i) -> p c t i", i=4),
+                out=woven.rearrange("p (c i t) -> p c t i", i=RUN, t=PACK),
+                in_=rows[:].rearrange("p t (c i) -> p c t i", i=RUN),
             )
 
-        def gather_x(rows, i, m0, width):
-            cols = slice(m0 // PER_COLUMN, (m0 + width) // PER_COLUMN)
-            nc.vector.tensor_copy(out=rows[:, i % PACK, :], in_=page[i][:].indirect(idx3[:, cols]))
-
         def quantize_x(woven, b, m0, width):
-            nc.vector.quantize_mx(
-                out=x_codes[b][:, m0 : m0 + width].bitcast(FP8X4), scales=x_scales[b][:, m0 : m0 + width], in_=woven[:]
+            cols = slice(m0, m0 + width)
+            nc.vector.quantize_mx(out=x_codes[b][:, cols].bitcast(FP8X4), scales=x_scales[b][:, cols], in_=woven)
+
+        def y_pass(banks, b, m0, width):
+            per_bank = BANK // width
+            cols = slice(m0, m0 + width)
+            for c in range(n_tiles):
+                nc.tensor.matmul_mx(
+                    out=banks[c // per_bank][:, c % per_bank, :],
+                    lhsT=w2_codes[:, b, 2 * P * c : 2 * P * (c + 1)].bitcast(FP4X4),
+                    lhsT_scale=w2_planes[:, b, P * c : P * (c + 1)],
+                    rhs=x_codes[b][:, cols].bitcast(FP8X4),
+                    rhs_scale=x_scales[b][:, cols],
+                    start=(b == 0 and c % per_bank == 0),
+                    stop=(b == r_passes - 1 and c % per_bank == per_bank - 1),
+                )
+
+        def finish(woven, banks, m0, width):
+            quantize_x(woven, r_passes - 1, m0, width)
+            y_pass(banks, r_passes - 1, m0, width)
+            piece = scores[:, n_tiles * m0 : n_tiles * (m0 + width)]
+            for n, y in enumerate(banks):
+                nc.scalar.activation(
+                    out=piece[:, n * BANK : (n + 1) * BANK], in_=y[:].rearrange("p c m -> p (c m)"), func=ACT.Tanh
+                )
+            nc.sync.dma_start(
+                out=out.rearrange("(c p) m -> p c m", p=P)[:, :, m0 : m0 + width],
+                in_=piece.rearrange("p (c m) -> p c m", m=width),
             )
 
         nc.vector.memset(table_scales[:].bitcast(I32), 0)
         nc.vector.memset(w2_planes[:].rearrange("p a n -> p (a n)").bitcast(I32), 0)
         nc.sync.dma_start(idx[:], offs)
         load_table(0)
-        for q in range(4):
-            nc.scalar.dma_start(
-                out=table_scales[32 * q : 32 * q + 4 * k_passes, :].bitcast(I32),
-                in_=tab_scales[:, 4 * q : 4 * q + 4, :].bitcast(I32),
+        for q in range(QUADRANTS):
+            nc.gpsimd.dma_start(
+                out=table_scales[32 * q : 32 * q + PACK * k_passes, :].bitcast(I32),
+                in_=tab_scales[:, PACK * q : PACK * (q + 1), :].bitcast(I32),
             )
-        raws = [load_w1(a, 0) for a in range(k_passes)]
-        load_table(1)
+        raws = load_w1(0)
         nc.sync.dma_start(idx2[:], offs2)
-        load_page(0)
-        load_page(1)
-        nc.sync.dma_start(idx3[:], offs3)
-        load_page(2)
-        load_page(3)
+        for i in range(EARLY_TILES):
+            load_page(i)
+        load_table(1)
 
-        nc.vector.tensor_copy(out=v_codes[0][:], in_=table[0][:].bitcast(U32).indirect(idx[:]))
+        gather_words(0, 0, S)
         nc.vector.tensor_copy(out=v_scales[:], in_=table_scales[:].indirect(idx[:]))
-        for a in range(k_passes):
-            quantize_w1(weave_w1(raws[a]), a, 0)
-        nc.vector.tensor_copy(out=v_codes[1][:], in_=table[1][:].bitcast(U32).indirect(idx[:]))
+        quantize_w1(raws, 0)
 
-        raws = [load_w1(a, 1) for a in range(k_passes)]
-        for i in range(PACK, page_tiles):
+        raws = load_w1(1)
+        nc.sync.dma_start(idx3[:], offs3)
+        for i in range(EARLY_TILES, page_tiles):
             load_page(i)
         nc.sync.dma_start(out=w2_codes[:].bitcast(I32), in_=w2_words.rearrange("a p c -> p a c").bitcast(I32))
-        for q in range(4):
+        for q in range(QUADRANTS):
             nc.sync.dma_start(
-                out=w2_planes[32 * q : 32 * q + 4, :, :].bitcast(I32),
-                in_=w2_scales[:, 4 * q : 4 * q + 4, :].rearrange("a r c -> r a c").bitcast(I32),
+                out=w2_planes[32 * q : 32 * q + PACK, :, :].bitcast(I32),
+                in_=w2_scales[:, PACK * q : PACK * (q + 1), :].rearrange("a s c -> s a c").bitcast(I32),
             )
 
-        def gather_old(i):
-            old = ring_tile(i, [P, S], F32, f"old{i}")
-            nc.vector.tensor_copy(out=old[:], in_=page[i][:].indirect(idx2[:]))
-            return old
+        olds = [gather_old(i) for i in range(page_tiles)]
+        for j0 in range(0, S, BANK):
+            gather_words(1, j0, BANK)
 
-        def raise_to_h(old, i):
-            b, t = divmod(i, PACK)
-            for j0 in range(0, S, BANK):
-                cols = slice(j0, j0 + BANK)
-                h = psum.tile([P, BANK], F32, name="h")
-                for a in range(k_passes):
-                    nc.tensor.matmul_mx(
-                        out=h[:],
-                        lhsT=w1_codes[a, b][:, t * P : (t + 1) * P].bitcast(FP8X4),
-                        lhsT_scale=w1_scales[a, b][:, t * P : (t + 1) * P],
-                        rhs=v_codes[a][:, cols].bitcast(FP8X4),
-                        rhs_scale=v_scales[4 * a :, cols],
-                        start=(a == 0),
-                        stop=(a == k_passes - 1),
-                    )
-                nc.vector.tensor_tensor(out=old[:, cols], in0=old[:, cols], in1=h[:], op=MAX)
+        x_rows_first = keep.tile([P, PACK, M], BF16, name="x_rows_first", tag="table0", align_bytes=ALIGN)
+        direct_first = [i for i in DIRECT_TILES if i < PACK]
+        direct_last = [i for i in DIRECT_TILES if i >= PACK]
+        for i in direct_first:
+            max_on_vector(i)
+        quantize_w1(raws, 1)
+        prepared = {i: make_masks(i) for i in masked_tiles[:2]}
+        chosen = {masked_tiles[0]: choose(masked_tiles[0], *prepared[masked_tiles[0]])}
+        for i in direct_first:
+            scatter(i, olds[i])
+        for n, i in enumerate(masked_tiles):
+            for ahead in masked_tiles[n + 2 : n + 3]:
+                prepared[ahead] = make_masks(ahead)
+            for ahead in masked_tiles[n + 1 : n + 2]:
+                chosen[ahead] = choose(ahead, *prepared[ahead])
+            if i == masked_tiles[-1]:
+                first_rows = keep.tile(
+                    [P, PACK, PIECES[0]], BF16, name="x_rows0", tag=chosen_tag(masked_tiles[-2]), align_bytes=ALIGN
+                )
+                for other in range(PACK, page_tiles):
+                    if other != i:
+                        gather_x(first_rows, other, 0, PIECES[0])
+            scatter(i, chosen[i])
+            if i == PACK - 1:
+                for direct in direct_last:
+                    max_on_vector(direct)
+                    scatter(direct, olds[direct])
+            if i == masked_tiles[-3]:
+                x_woven_first = keep.tile(
+                    [P, PACK * M], BF16, name="x_woven_first", tag=take_tag(masked_tiles[-2]), align_bytes=ALIGN
+                )
+                weave_x(x_woven_first[:], x_rows_first)
+                quantize_x(x_woven_first[:], 0, 0, M)
 
-        olds = {0: gather_old(0)}
-        for i in range(page_tiles):
-            if i + 1 < page_tiles:
-                olds[i + 1] = gather_old(i + 1)
-            raise_to_h(olds[i], i)
-            if 1 <= i <= PACK:
-                gather_x(x_rows_first, i - 1, 0, NX)
-            if i == PACK:
-                weave_x(x_woven_first, x_rows_first)
-            nc.vector.tensor_copy(out=page[i][:].indirect(idx2[:]), in_=olds[i][:])
-            if i == 1:
-                for a in range(k_passes):
-                    quantize_w1(weave_w1(raws[a]), a, 1)
-            if i == PACK + 1:
-                quantize_x(x_woven_first, 0, 0, NX)
-
-        out_v = out.rearrange("(c p) m -> p c m", p=P)
-
-        def finish(woven, m0, width):
-            quantize_x(woven, r_passes - 1, m0, width)
-            per_bank = BANK // width
-            res = stage.tile([P, n_tiles, width], F32, name="res", bufs=3)
-            for c0 in range(0, n_tiles, per_bank):
-                y = psum.tile([P, per_bank, width], F32, name="y")
-                for c in range(c0, c0 + per_bank):
-                    for b in range(r_passes):
-                        nc.tensor.matmul_mx(
-                            out=y[:, c - c0, :],
-                            lhsT=w2_codes[:, b, 2 * P * c : 2 * P * (c + 1)].bitcast(FP4X4),
-                            lhsT_scale=w2_planes[:, b, P * c : P * (c + 1)],
-                            rhs=x_codes[b][:, m0 : m0 + width].bitcast(FP8X4),
-                            rhs_scale=x_scales[b][:, m0 : m0 + width],
-                            start=(b == 0),
-                            stop=(b == r_passes - 1),
-                        )
-                nc.scalar.activation(out=res[:, c0 : c0 + per_bank, :], in_=y[:], func=TANH)
-            nc.sync.dma_start(out=out_v[:, :, m0 : m0 + width], in_=res[:])
-
-        first_slot = page_tiles - 2
-        waiting = None
-        m0 = 0
+        x_woven_last = keep.tile([P, PACK * M], BF16, name="x_woven_last", tag="table0", align_bytes=ALIGN)
+        scores = keep.tile([P, n_tiles * M], F32, name="scores", tag="table1", align_bytes=ALIGN)
+        starts = [sum(PIECES[:n]) for n in range(len(PIECES))]
+        y_banks = []
         for n, width in enumerate(PIECES):
-            rows = ring_tile(first_slot - 2 * n, [P, PACK, width], BF16, f"x_rows{n}")
-            for i in range(PACK, page_tiles):
-                gather_x(rows, i, m0, width)
+            per_bank = BANK // width
+            banks = [
+                psum.tile([P, per_bank, width], F32, name=f"y{n}{c}", tag="bank") for c in range(0, n_tiles, per_bank)
+            ]
+            y_pass(banks, 0, starts[n], width)
+            y_banks.append(banks)
+
+        waiting = None
+        for n, width in enumerate(PIECES):
+            if n == 0:
+                rows = first_rows
+                gather_x(rows, masked_tiles[-1], 0, width)
+            else:
+                rows = keep.tile(
+                    [P, PACK, width], BF16, name=f"x_rows{n}", tag=chosen_tag(masked_tiles[n % 2 - 2]), align_bytes=ALIGN
+                )
+                for i in range(PACK, page_tiles):
+                    gather_x(rows, i, starts[n], width)
+            woven = x_woven_last[:, PACK * starts[n] : PACK * (starts[n] + width)]
+            weave_x(woven, rows)
             if waiting is not None:
                 finish(*waiting)
-            woven = ring_tile(first_slot - 2 * n - 1, [P, PACK * width], BF16, f"x_woven{n}")
-            weave_x(woven, rows)
-            waiting = (woven, m0, width)
-            m0 = m0 + width
+            waiting = (woven, y_banks[n], starts[n], width)
         finish(*waiting)

from contextlib import ExitStack

import concourse.mybir as mybir

T, S, T2, M, K, H, N = 4096, 1024, 2048, 1024, 1024, 1024, 512
FLOPS = 2 * K * H * S + 2 * H * N * M

F32 = mybir.dt.float32
BF16 = mybir.dt.bfloat16
I32 = mybir.dt.int32
U32 = mybir.dt.uint32
U16 = mybir.dt.uint16
U8 = mybir.dt.uint8
FP8X4 = mybir.dt.float8_e4m3fn_x4
FP4X4 = mybir.dt.float4_e2m1fn_x4
ALU = mybir.AluOpType
ACT = mybir.ActivationFunctionType

P = 128
PACK = 4
PASS = P * PACK
BANK = 512
QUADRANTS = 4
PER_COLUMN = 16
ALIGN = 64

DIRECT_TILES = (0, 1, 4)
EARLY_TILES = 6
PIECES = (256, 256, 128, 128, 128, 128)
RUN = 4
H_COPIES = 3
CHOSEN_RING = 3
TAKE_RING = 2


def tile_list_bearing_seizure_step_kernel(
    tc, tab_words, tab_scales, offs, w1, page0, offs2, offs3, w2_words, w2_scales, out
):
    nc = tc.nc
    k_passes = K // PASS
    r_passes = H // PASS
    n_tiles = N // P
    page_tiles = r_passes * PACK
    masked_tiles = [i for i in range(page_tiles) if i not in DIRECT_TILES]

    with ExitStack() as ctx:
        keep = ctx.enter_context(tc.tile_pool(name="keep", bufs=1))
        stage = ctx.enter_context(tc.tile_pool(name="stage", bufs=2))
        psum = ctx.enter_context(tc.psum_pool(name="psum", bufs=8))

        idx = keep.tile([P, S // PER_COLUMN], U16, name="idx")
        idx2 = keep.tile([P, S // PER_COLUMN], U16, name="idx2")
        idx3 = keep.tile([P, M // PER_COLUMN], U16, name="idx3")
        table = [keep.tile([P, T], I32, name=f"table{a}", tag=f"table{a}", align_bytes=ALIGN) for a in range(k_passes)]
        table_scales = keep.tile([P, T], U8, name="table_scales", align_bytes=ALIGN)
        v_codes = [keep.tile([P, S], U32, name=f"v_codes{a}", align_bytes=ALIGN) for a in range(k_passes)]
        v_scales = keep.tile([P, S], U8, name="v_scales", align_bytes=ALIGN)
        w1_codes = [keep.tile([P, k_passes * PASS], U32, name=f"w1_codes{b}", align_bytes=ALIGN) for b in range(r_passes)]
        w1_scales = [keep.tile([P, k_passes * PASS], U8, name=f"w1_scales{b}", align_bytes=ALIGN) for b in range(r_passes)]
        page = [keep.tile([P, T2], F32, name=f"page{i}", align_bytes=ALIGN) for i in range(page_tiles)]
        w2_codes = keep.tile([P, r_passes, 2 * N], U8, name="w2_codes", align_bytes=ALIGN)
        w2_planes = keep.tile([P, r_passes, N], U8, name="w2_planes", align_bytes=ALIGN)
        x_codes = [keep.tile([P, M], U32, name=f"x_codes{b}", align_bytes=ALIGN) for b in range(r_passes)]
        x_scales = [keep.tile([P, M], U8, name=f"x_scales{b}", align_bytes=ALIGN) for b in range(r_passes)]

        def chosen_tag(i):
            return f"chosen{masked_tiles.index(i) % CHOSEN_RING}"

        def take_tag(i):
            return f"take{masked_tiles.index(i) % TAKE_RING}"

        def entries(lst, first, count):
            return lst[:, first // PER_COLUMN : (first + count) // PER_COLUMN]

        def load_table(a):
            nc.sync.dma_start(out=table[a][:], in_=tab_words[a].rearrange("p t i -> p (t i)").bitcast(I32))

        def load_page(i):
            b, t = divmod(i, PACK)
            rows = page0[b * PASS : (b + 1) * PASS, :].rearrange("(p t) c -> p t c", t=PACK)
            nc.sync.dma_start(out=page[i][:], in_=rows[:, t, :])

        def load_w1(b):
            raws = []
            for a in range(k_passes):
                raw = stage.tile([P, PACK, PASS], F32, name="w1_raw", align_bytes=ALIGN)
                block = w1[a * PASS : (a + 1) * PASS, b * PASS : (b + 1) * PASS]
                nc.sync.dma_start(out=raw[:], in_=block.rearrange("(p j) c -> p j c", j=PACK))
                raws.append(raw)
            return raws

        def quantize_w1(raws, b):
            woven = keep.tile([P, k_passes * PASS * PACK], BF16, name=f"w1_woven{b}", tag="w1_woven", align_bytes=ALIGN)
            for a, raw in enumerate(raws):
                nc.scalar.copy(
                    out=woven[:, a * PASS * PACK : (a + 1) * PASS * PACK].rearrange("p (t m j) -> p m j t", t=PACK, j=PACK),
                    in_=raw[:].rearrange("p j (m t) -> p m j t", t=PACK),
                )
            nc.vector.quantize_mx(out=w1_codes[b][:].bitcast(FP8X4), scales=w1_scales[b][:], in_=woven[:])

        def gather_words(a, j0, count):
            nc.vector.tensor_copy(
                out=v_codes[a][:, j0 : j0 + count], in_=table[a][:].bitcast(U32).indirect(entries(idx, j0, count))
            )

        def gather_old(i):
            old = keep.tile([P, S], F32, name=f"old{i}", align_bytes=ALIGN)
            nc.vector.tensor_copy(out=old[:], in_=page[i][:].indirect(idx2[:]))
            return old

        def h_banks(i):
            b, t = divmod(i, PACK)
            banks = []
            for j0 in range(0, S, BANK):
                cols = slice(j0, j0 + BANK)
                h = psum.tile([P, BANK], F32, name="h", tag="bank")
                for a in range(k_passes):
                    w1_cols = slice(a * PASS + t * P, a * PASS + (t + 1) * P)
                    nc.tensor.matmul_mx(
                        out=h[:],
                        lhsT=w1_codes[b][:, w1_cols].bitcast(FP8X4),
                        lhsT_scale=w1_scales[b][:, w1_cols],
                        rhs=v_codes[a][:, cols].bitcast(FP8X4),
                        rhs_scale=v_scales[PACK * a :, cols],
                        start=(a == 0),
                        stop=(a == k_passes - 1),
                    )
                banks.append((cols, h))
            return banks

        def max_on_vector(i):
            for cols, h in h_banks(i):
                nc.vector.tensor_tensor(out=olds[i][:, cols], in0=olds[i][:, cols], in1=h[:], op=ALU.max)

        def make_masks(i):
            h_copy = stage.tile([P, S], F32, name="h_copy", bufs=H_COPIES)
            for cols, h in h_banks(i):
                nc.scalar.copy(out=h_copy[:, cols], in_=h[:])
            take = keep.tile([P, S], F32, name=f"take{i}", tag=take_tag(i), align_bytes=ALIGN)
            stay = stage.tile([P, S], F32, name="stay")
            nc.gpsimd.tensor_tensor(out=take[:], in0=h_copy[:], in1=olds[i][:], op=ALU.subtract)
            nc.scalar.activation(out=take[:], in_=take[:], func=ACT.Sign)
            nc.scalar.activation(out=take[:], in_=take[:], func=ACT.Relu)
            nc.scalar.activation(out=stay[:], in_=take[:], func=ACT.Identity, scale=-1.0, bias=1.0)
            return h_copy, take, stay

        def choose(i, h_copy, take, stay):
            nc.gpsimd.tensor_tensor(out=h_copy[:], in0=h_copy[:], in1=take[:], op=ALU.mult)
            nc.gpsimd.tensor_tensor(out=olds[i][:], in0=olds[i][:], in1=stay[:], op=ALU.mult)
            chosen = keep.tile([P, S], F32, name=f"chosen{i}", tag=chosen_tag(i), align_bytes=ALIGN)
            nc.gpsimd.tensor_tensor(out=chosen[:], in0=h_copy[:], in1=olds[i][:], op=ALU.add)
            return chosen

        def gather_x(rows, i, m0, width):
            nc.vector.tensor_copy(out=rows[:, i % PACK, :], in_=page[i][:].indirect(entries(idx3, m0, width)))

        def scatter(i, values):
            nc.vector.tensor_copy(out=page[i][:].indirect(idx2[:]), in_=values[:])
            if i < PACK:
                gather_x(x_rows_first, i, 0, M)

        def weave_x(woven, rows):
            nc.scalar.copy(
                out=woven.rearrange("p (c i t) -> p c t i", i=RUN, t=PACK),
                in_=rows[:].rearrange("p t (c i) -> p c t i", i=RUN),
            )

        def quantize_x(woven, b, m0, width):
            cols = slice(m0, m0 + width)
            nc.vector.quantize_mx(out=x_codes[b][:, cols].bitcast(FP8X4), scales=x_scales[b][:, cols], in_=woven)

        def y_pass(banks, b, m0, width):
            per_bank = BANK // width
            cols = slice(m0, m0 + width)
            for c in range(n_tiles):
                nc.tensor.matmul_mx(
                    out=banks[c // per_bank][:, c % per_bank, :],
                    lhsT=w2_codes[:, b, 2 * P * c : 2 * P * (c + 1)].bitcast(FP4X4),
                    lhsT_scale=w2_planes[:, b, P * c : P * (c + 1)],
                    rhs=x_codes[b][:, cols].bitcast(FP8X4),
                    rhs_scale=x_scales[b][:, cols],
                    start=(b == 0 and c % per_bank == 0),
                    stop=(b == r_passes - 1 and c % per_bank == per_bank - 1),
                )

        def finish(woven, banks, m0, width):
            quantize_x(woven, r_passes - 1, m0, width)
            y_pass(banks, r_passes - 1, m0, width)
            piece = scores[:, n_tiles * m0 : n_tiles * (m0 + width)]
            for n, y in enumerate(banks):
                nc.scalar.activation(
                    out=piece[:, n * BANK : (n + 1) * BANK], in_=y[:].rearrange("p c m -> p (c m)"), func=ACT.Tanh
                )
            nc.sync.dma_start(
                out=out.rearrange("(c p) m -> p c m", p=P)[:, :, m0 : m0 + width],
                in_=piece.rearrange("p (c m) -> p c m", m=width),
            )

        nc.vector.memset(table_scales[:].bitcast(I32), 0)
        nc.vector.memset(w2_planes[:].rearrange("p a n -> p (a n)").bitcast(I32), 0)
        nc.sync.dma_start(idx[:], offs)
        load_table(0)
        for q in range(QUADRANTS):
            nc.gpsimd.dma_start(
                out=table_scales[32 * q : 32 * q + PACK * k_passes, :].bitcast(I32),
                in_=tab_scales[:, PACK * q : PACK * (q + 1), :].bitcast(I32),
            )
        raws = load_w1(0)
        nc.sync.dma_start(idx2[:], offs2)
        for i in range(EARLY_TILES):
            load_page(i)
        load_table(1)

        gather_words(0, 0, S)
        nc.vector.tensor_copy(out=v_scales[:], in_=table_scales[:].indirect(idx[:]))
        quantize_w1(raws, 0)

        raws = load_w1(1)
        nc.sync.dma_start(idx3[:], offs3)
        for i in range(EARLY_TILES, page_tiles):
            load_page(i)
        nc.sync.dma_start(out=w2_codes[:].bitcast(I32), in_=w2_words.rearrange("a p c -> p a c").bitcast(I32))
        for q in range(QUADRANTS):
            nc.sync.dma_start(
                out=w2_planes[32 * q : 32 * q + PACK, :, :].bitcast(I32),
                in_=w2_scales[:, PACK * q : PACK * (q + 1), :].rearrange("a s c -> s a c").bitcast(I32),
            )

        olds = [gather_old(i) for i in range(page_tiles)]
        for j0 in range(0, S, BANK):
            gather_words(1, j0, BANK)

        x_rows_first = keep.tile([P, PACK, M], BF16, name="x_rows_first", tag="table0", align_bytes=ALIGN)
        direct_first = [i for i in DIRECT_TILES if i < PACK]
        direct_last = [i for i in DIRECT_TILES if i >= PACK]
        for i in direct_first:
            max_on_vector(i)
        quantize_w1(raws, 1)
        prepared = {i: make_masks(i) for i in masked_tiles[:2]}
        chosen = {masked_tiles[0]: choose(masked_tiles[0], *prepared[masked_tiles[0]])}
        for i in direct_first:
            scatter(i, olds[i])
        for n, i in enumerate(masked_tiles):
            for ahead in masked_tiles[n + 2 : n + 3]:
                prepared[ahead] = make_masks(ahead)
            for ahead in masked_tiles[n + 1 : n + 2]:
                chosen[ahead] = choose(ahead, *prepared[ahead])
            if i == masked_tiles[-1]:
                first_rows = keep.tile(
                    [P, PACK, PIECES[0]], BF16, name="x_rows0", tag=chosen_tag(masked_tiles[-2]), align_bytes=ALIGN
                )
                for other in range(PACK, page_tiles):
                    if other != i:
                        gather_x(first_rows, other, 0, PIECES[0])
            scatter(i, chosen[i])
            if i == PACK - 1:
                for direct in direct_last:
                    max_on_vector(direct)
                    scatter(direct, olds[direct])
            if i == masked_tiles[-3]:
                x_woven_first = keep.tile(
                    [P, PACK * M], BF16, name="x_woven_first", tag=take_tag(masked_tiles[-2]), align_bytes=ALIGN
                )
                weave_x(x_woven_first[:], x_rows_first)
                quantize_x(x_woven_first[:], 0, 0, M)

        x_woven_last = keep.tile([P, PACK * M], BF16, name="x_woven_last", tag="table0", align_bytes=ALIGN)
        scores = keep.tile([P, n_tiles * M], F32, name="scores", tag="table1", align_bytes=ALIGN)
        starts = [sum(PIECES[:n]) for n in range(len(PIECES))]
        y_banks = []
        for n, width in enumerate(PIECES):
            per_bank = BANK // width
            banks = [
                psum.tile([P, per_bank, width], F32, name=f"y{n}{c}", tag="bank") for c in range(0, n_tiles, per_bank)
            ]
            y_pass(banks, 0, starts[n], width)
            y_banks.append(banks)

        waiting = None
        for n, width in enumerate(PIECES):
            if n == 0:
                rows = first_rows
                gather_x(rows, masked_tiles[-1], 0, width)
            else:
                rows = keep.tile(
                    [P, PACK, width], BF16, name=f"x_rows{n}", tag=chosen_tag(masked_tiles[n % 2 - 2]), align_bytes=ALIGN
                )
                for i in range(PACK, page_tiles):
                    gather_x(rows, i, starts[n], width)
            woven = x_woven_last[:, PACK * starts[n] : PACK * (starts[n] + width)]
            weave_x(woven, rows)
            if waiting is not None:
                finish(*waiting)
            waiting = (woven, y_banks[n], starts[n], width)
        finish(*waiting)
